import numpy as np
import ml_dtypes


def mxq(x, axis, fmt="e4m3"):
    dtype, down = {"e4m3": (ml_dtypes.float8_e4m3fn, 7), "e5m2": (ml_dtypes.float8_e5m2, 14)}[fmt]
    v = np.moveaxis(np.asarray(x, np.float32).astype(ml_dtypes.bfloat16).astype(np.float64), axis, -1)
    blocks = v.reshape(v.shape[:-1] + (-1, 32))
    amax = np.abs(blocks).max(-1, keepdims=True)
    byte = np.maximum(np.where(amax > 0, np.frexp(amax)[1] - 1 + 127, 0) - down, 1)
    scale = np.exp2(byte - 127.0)
    codes = (blocks / scale).astype(np.float32).astype(dtype).astype(np.float64)
    return np.moveaxis((codes * scale).reshape(v.shape), -1, axis)


WIDE = False


def mx_kscale(k):
    if not WIDE:
        return np.ones(k)
    levels = np.array([10, -10, 5, -5, 0])
    if k % 512:
        return np.exp2(np.random.permutation(np.resize(levels, k // 32))).repeat(32)
    a = np.empty((k // 512, 16))
    for p in range(k // 512):
        a[p, :8] = np.random.permutation(np.resize(levels, 8))
        for g in range(8):
            far = levels[np.abs(levels - a[p, g]) >= 10]
            a[p, g + 8] = far[np.random.randint(len(far))]
    return np.exp2(a.ravel()).repeat(32)


def f64(x):
    return np.asarray(x).astype(np.float64)


def striped(idx):
    return np.tile(idx.reshape(-1, 16).T, (8, 1)).astype(np.uint16)


def unstriped(offs):
    return offs[:16].T.reshape(-1).astype(np.int64)


def striped8(idx):
    return np.concatenate([x.reshape(-1, 16).T for x in idx]).astype(np.uint16)


def runs(offs, k):
    lists = np.stack([offs[16 * r : 16 * r + 16].T.reshape(-1) for r in range(8)]).astype(np.int64)
    return lists[np.arange(k) % 512 // 64]


def pack_weight(w):
    k, n = w.shape
    w = f64(np.asarray(w, np.float32).astype(ml_dtypes.bfloat16)).reshape(k // 32, 32, n)
    amax = np.abs(w).max(1)
    byte = np.clip(np.where(amax > 0, np.frexp(amax)[1] - 1 + 127 - 7, 1), 1, 254)
    scaled = (w * np.exp2(127.0 - byte)[:, None, :]).reshape(k, n).astype(np.float32)
    words = np.ascontiguousarray(scaled.reshape(k // 512, 128, 4, n).transpose(0, 1, 3, 2)).astype(ml_dtypes.float8_e4m3fn).view(np.uint8)
    return words, np.ascontiguousarray(byte.astype(np.uint8).reshape(k // 512, 16, n))


def unpack_weight(words, scales):
    g, p, n, _ = words.shape
    vals = np.ascontiguousarray(words).view(ml_dtypes.float8_e4m3fn).astype(np.float64) * np.repeat(np.exp2(scales.astype(np.float64) - 127.0), 8, axis=1)[..., None]
    return vals.transpose(0, 1, 3, 2).reshape(g * 512, n)


K, T, S, N, H, W, G = 512, 2048, 512, 512, 512, 256, 2048


def setup_inputs():
    n = np.random.standard_normal
    s = mx_kscale(K)[:, None]
    u = mx_kscale(H)
    packed_xT = pack_weight(n((K, T)) * s)
    perm = np.stack([np.random.permutation(S) for _ in range(8)])
    return {
        "x_words": packed_xT[0],
        "x_scales": packed_xT[1],
        "w1": (n((K, H)) / np.sqrt(K) / s).astype(np.float32),
        "gn": (np.random.uniform(0.5, 1.5, (H, 1)) * u[:, None]).astype(np.float32),
        "w2": (n((H, N)) / np.sqrt(2 * H) / u[:, None]).astype(np.float32),
        "w3": (n((K, N)) / np.sqrt(2 * K) / s).astype(np.float32),
        "offs": striped8(np.random.randint(0, T, (8, S))),
        "n1": striped8(perm[:, :W]),
        "n2": striped8(perm[:, W:]),
        "two": striped(np.random.permutation(T)[:S]),
        "n3": striped(np.random.randint(0, S, G)),
    }


def reference(x_words, x_scales, w1, gn, w2, w3, offs, n1, n2, two, n3):
    xq = unpack_weight(x_words, x_scales)[np.arange(K)[:, None], runs(offs, K)]
    y = mxq(f64(w1), 0, "e4m3").T @ xq
    pa = y[np.arange(H)[:, None], runs(n1, H)]
    pb = y[np.arange(H)[:, None], runs(n2, H)]
    rb = np.maximum(0.5 * pa, pb)
    ra = pb - pa
    ds = np.zeros((H, S))
    ds[np.arange(H)[:, None], runs(n1, H)] = ra
    dt = ds.copy()
    dt[np.arange(H)[:, None], runs(n2, H)] = rb
    z = f64(gn) * dt
    x_two = unpack_weight(x_words, x_scales)[:, unstriped(two)]
    h = mxq(f64(w2), 0, "e4m3").T @ mxq(z, 0, "e4m3") + mxq(f64(w3), 0, "e4m3").T @ x_two
    ex = np.exp(h)
    mb = ex[:, unstriped(n3)]
    ms = mb.reshape(N, S, 4).sum(axis=2)
    return np.log(ms + ex) - h

@@ -1,0 +1,267 @@
+from contextlib import ExitStack
+
+import concourse.mybir as mybir
+
+K, T, S, N, H, W, G = 512, 2048, 512, 512, 512, 256, 2048
+P = 128
+PACK = 4
+FLOPS = 2 * (K * H * S + H * N * S + K * N * S)
+
+F32 = mybir.dt.float32
+BF16 = mybir.dt.bfloat16
+I32 = mybir.dt.int32
+U32 = mybir.dt.uint32
+U16 = mybir.dt.uint16
+U8 = mybir.dt.uint8
+FP8X4 = mybir.dt.float8_e4m3fn_x4
+ACT = mybir.ActivationFunctionType
+ALU = mybir.AluOpType
+
+HALF = S // 2
+MEMBERS = G // S
+
+
+def tile_picked_hmixliftglse_none_p_kernel(
+    tc, x_words, x_scales, w1, gn, w2, w3, offs, n1, n2, two, n3, out
+):
+    nc = tc.nc
+    with ExitStack() as ctx:
+        lists = ctx.enter_context(tc.tile_pool(name="lists", bufs=1))
+        sb = ctx.enter_context(tc.tile_pool(name="sb", bufs=1))
+        psum = ctx.enter_context(tc.psum_pool(name="psum", bufs=1))
+
+        def load_list(src, name):
+            t = lists.tile(list(src.shape), U16, name=name)
+            nc.sync.dma_start(t[:], src)
+            return t
+
+        l_offs = load_list(offs, "l_offs")
+        xs = sb.tile([P, T], U8, name="xs", align_bytes=64)
+        nc.sync.dma_start(
+            xs[:].bitcast(I32),
+            x_scales[0].bitcast(I32).unsqueeze(1).to_broadcast([16, 8, T // 4]),
+        )
+        l_two = load_list(two, "l_two")
+        l_n1 = load_list(n1, "l_n1")
+        l_n2 = load_list(n2, "l_n2")
+        xw = sb.tile([P, T], I32, name="xw", align_bytes=64)
+        nc.sync.dma_start(xw[:], x_words[0].rearrange("p n t -> p (n t)").bitcast(I32))
+        w1_rows = w1.rearrange("(p j) c -> p j c", j=PACK)
+        w1_raw = []
+        for u in range(2):
+            t = sb.tile([P, PACK, H // 2], F32, name="w1_raw%d" % u, tag="w1_raw%d" % u)
+            nc.sync.dma_start(t[:], w1_rows[:, :, u * (H // 2) : (u + 1) * (H // 2)])
+            w1_raw.append(t)
+        l_n3 = load_list(n3, "l_n3")
+
+        def pick_scales(lst, name, queue):
+            placed = sb.tile([P, S], U8, name=name + "_placed", align_bytes=64)
+            nc.gpsimd.memset(placed[:], 0)
+            picked = sb.tile([P, S], U8, name=name + "_picked", tag=name + "_late", align_bytes=64)
+            nc.vector.tensor_copy(picked[:], xs[:].indirect(lst[:]))
+            for r in range(4):
+                queue.dma_start(
+                    placed[r:P:32, :].bitcast(I32), picked[8 * r : P : 32, :].bitcast(I32)
+                )
+            return placed
+
+        def pick_words(lst, name):
+            picked = sb.tile([P, S], U32, name=name, align_bytes=64)
+            nc.vector.tensor_copy(picked[:], xw[:].bitcast(U32).indirect(lst[:]))
+            return picked
+
+        xq_scales = pick_scales(l_offs, "xq_s", nc.scalar)
+        x2_scales = pick_scales(l_two, "x2_s", nc.sync)
+        w3_raw = sb.tile([P, PACK, N], F32, name="w3_raw", tag="xq_s_late", align_bytes=64)
+        nc.sync.dma_start(w3_raw[:], w3.rearrange("(p j) c -> p j c", j=PACK))
+        w2_raw = sb.tile([P, PACK, N], F32, name="w2_raw", tag="x2_s_late", align_bytes=64)
+        nc.sync.dma_start(w2_raw[:], w2.rearrange("(p j) c -> p j c", j=PACK))
+        xq_words = pick_words(l_offs, "xq_words")
+
+        w1_bf = sb.tile([P, PACK, P, PACK], BF16, name="w1_bf", align_bytes=64)
+        for u, copy in enumerate((nc.scalar.copy, nc.vector.tensor_copy)):
+            copy(
+                w1_bf[:, :, u * 64 : (u + 1) * 64, :].rearrange("p t m j -> p m t j"),
+                w1_raw[u][:].rearrange("p j (m t) -> p m t j", t=PACK),
+            )
+        gain = sb.tile([P, PACK], F32, name="gain", tag="w1_raw0")
+        nc.sync.dma_start(gain[:], gn.rearrange("(p t) o -> p (t o)", t=PACK))
+        w1_codes = sb.tile([P, H], U32, name="w1_codes", align_bytes=64)
+        w1_scales = sb.tile([P, H], U8, name="w1_scales", align_bytes=64)
+        w1_flat = w1_bf[:].rearrange("p t m j -> p (t m j)")
+        for a, b in ((0, P), (P, H)):
+            nc.vector.quantize_mx(
+                out=w1_codes[:, a:b].bitcast(FP8X4),
+                scales=w1_scales[:, a:b],
+                in_=w1_flat[:, PACK * a : PACK * b],
+            )
+        x2_words = pick_words(l_two, "x2_words")
+
+        neg_pa, pb = [], []
+        for t in range(PACK):
+            acc = psum.tile([P, S], F32, name="y_acc%d" % t)
+            nc.tensor.matmul_mx(
+                out=acc[:],
+                lhsT=w1_codes[:, t * P : (t + 1) * P].bitcast(FP8X4),
+                lhsT_scale=w1_scales[:, t * P : (t + 1) * P],
+                rhs=xq_words[:].bitcast(FP8X4),
+                rhs_scale=xq_scales[:],
+                start=True,
+                stop=True,
+            )
+            y = sb.tile([P, S], F32, name="y%d" % t)
+            nc.scalar.copy(y[:], acc[:])
+            a = sb.tile([P, W], F32, name="neg_pa%d" % t)
+            b = sb.tile([P, W], F32, name="pb%d" % t)
+            nc.scalar.activation(a[:], y[:].indirect(l_n1[:]), ACT.Copy, scale=-1.0)
+            if t == 0:
+                nc.vector.tensor_copy(b[:], y[:].indirect(l_n2[:]))
+            else:
+                nc.scalar.activation(b[:], y[:].indirect(l_n2[:]), ACT.Copy)
+            neg_pa.append(a)
+            pb.append(b)
+
+        def round_weight(raw, name):
+            bf = sb.tile([P, N, PACK], BF16, name=name + "_bf", align_bytes=64)
+            nc.scalar.copy(
+                bf[:].rearrange("p (c i) j -> p c j i", i=4),
+                raw[:].rearrange("p j (c i) -> p c j i", i=4),
+            )
+            return bf
+
+        def quantize_weight(bf, name):
+            codes = sb.tile([P, N], U32, name=name + "_codes", align_bytes=64)
+            scales = sb.tile([P, N], U8, name=name + "_scales", align_bytes=64)
+            nc.vector.quantize_mx(
+                out=codes[:].bitcast(FP8X4), scales=scales[:], in_=bf[:].rearrange("p c j -> p (c j)")
+            )
+            return codes, scales
+
+        w3_bf = round_weight(w3_raw, "w3")
+        w2_bf = round_weight(w2_raw, "w2")
+
+        dt = [sb.tile([P, S], F32, name="dt%d" % t) for t in range(PACK)]
+        rb = [sb.tile([P, W], F32, name="rb%d" % t) for t in range(PACK)]
+        z_pairs = [sb.tile([P, 2, HALF, 2], BF16, name="z_pairs%d" % u, tag="z_pairs%d" % u, align_bytes=64) for u in range(2)]
+
+        def put_ra(t):
+            nc.vector.scalar_tensor_tensor(rb[t][:], neg_pa[t][:], -0.5, pb[t][:], ALU.mult, ALU.max)
+            nc.vector.tensor_tensor(dt[t][:].indirect(l_n1[:]), pb[t][:], neg_pa[t][:], ALU.add)
+
+        def put_rb(t):
+            nc.vector.tensor_copy(dt[t][:].indirect(l_n2[:]), rb[t][:])
+            for u in range(2):
+                nc.scalar.activation(
+                    z_pairs[u][:, t // 2, :, t % 2],
+                    dt[t][:, u * HALF : (u + 1) * HALF],
+                    ACT.Copy,
+                    scale=gain[:, t : t + 1],
+                )
+
+        put_ra(0)
+        for t in range(1, PACK):
+            put_ra(t)
+            put_rb(t - 1)
+        put_rb(PACK - 1)
+
+        w3_codes, w3_scales = quantize_weight(w3_bf, "w3")
+        w2_flat = w2_bf[:].rearrange("p c j -> p (c j)")
+        w2_first = sb.tile([P, P], U32, name="w2_first", align_bytes=64)
+        w2_scales = sb.tile([P, N], U8, name="w2_scales", align_bytes=64)
+        nc.vector.quantize_mx(out=w2_first[:].bitcast(FP8X4), scales=w2_scales[:, 0:P], in_=w2_flat[:, 0 : PACK * P])
+
+        z_bf = [sb.tile([P, HALF, PACK], BF16, name="z_bf%d" % u, align_bytes=64) for u in range(2)]
+        z_codes = [sb.tile([P, HALF], U32, name="z_codes%d" % u, align_bytes=64) for u in range(2)]
+        z_scales = [sb.tile([P, HALF], U8, name="z_scales%d" % u, align_bytes=64) for u in range(2)]
+        for u in range(2):
+            nc.vector.tensor_copy(
+                z_bf[u][:].rearrange("p j t -> p (j t)").bitcast(F32).rearrange("p (j h) -> p j h", h=2),
+                z_pairs[u][:].rearrange("p h j e -> p h (j e)").bitcast(F32).rearrange("p h j -> p j h"),
+            )
+        for u in range(2):
+            nc.vector.quantize_mx(
+                out=z_codes[u][:].bitcast(FP8X4),
+                scales=z_scales[u][:],
+                in_=z_bf[u][:].rearrange("p j t -> p (j t)"),
+            )
+
+        w2_rest = sb.tile([P, N - P], U32, name="w2_rest", tag="z_pairs1", align_bytes=64)
+        nc.vector.quantize_mx(out=w2_rest[:].bitcast(FP8X4), scales=w2_scales[:, P:N], in_=w2_flat[:, PACK * P :])
+        w2_codes = [w2_first[:]] + [w2_rest[:, i * P : (i + 1) * P] for i in range(3)]
+
+        h_acc = [psum.tile([P, S], F32, name="h_acc%d" % m) for m in range(4)]
+        for m in range(4):
+            nc.tensor.matmul_mx(
+                out=h_acc[m][:],
+                lhsT=w3_codes[:, m * P : (m + 1) * P].bitcast(FP8X4),
+                lhsT_scale=w3_scales[:, m * P : (m + 1) * P],
+                rhs=x2_words[:].bitcast(FP8X4),
+                rhs_scale=x2_scales[:],
+                start=True,
+                stop=False,
+            )
+            for u in range(2):
+                nc.tensor.matmul_mx(
+                    out=h_acc[m][:, u * HALF : (u + 1) * HALF],
+                    lhsT=w2_codes[m].bitcast(FP8X4),
+                    lhsT_scale=w2_scales[:, m * P : (m + 1) * P],
+                    rhs=z_codes[u][:].bitcast(FP8X4),
+                    rhs_scale=z_scales[u][:],
+                    start=False,
+                    stop=(u == 1),
+                )
+
+        ex = [sb.tile([P, S], F32, name="ex%d" % m) for m in range(4)]
+        inv_ex = [sb.tile([P, S], F32, name="inv_ex%d" % m) for m in range(4)]
+        mb = [sb.tile([P, G], F32, name="mb%d" % m) for m in range(4)]
+        pair = [sb.tile([P, S, 2], F32, name="pair%d" % m) for m in range(4)]
+        ms = [sb.tile([P, S], F32, name="ms%d" % m) for m in range(4)]
+        ratio = [sb.tile([P, S], F32, name="ratio%d" % m) for m in range(4)]
+        res = [sb.tile([P, S], F32, name="res%d" % m) for m in range(4)]
+
+        for m in range(4):
+            nc.scalar.activation(ex[m][:], h_acc[m][:], ACT.Exp)
+        for m in range(4):
+            nc.scalar.activation(inv_ex[m][:], h_acc[m][:], ACT.Exp, scale=-1.0)
+
+        def fetch(m, cols, on_vector):
+            for a, b in cols:
+                dst = mb[m][:, 16 * a : 16 * b]
+                src = ex[m][:].indirect(l_n3[:, a:b])
+                if on_vector:
+                    nc.vector.tensor_copy(dst, src)
+                else:
+                    nc.scalar.activation(dst, src, ACT.Copy)
+
+        def sums(m, parts):
+            members = mb[m][:].rearrange("p (j t) -> p j t", t=MEMBERS)
+            for js in parts:
+                nc.vector.tensor_tensor(pair[m][:, js, :], members[:, js, 0:2], members[:, js, 2:4], ALU.add)
+            for js in parts:
+                nc.vector.tensor_tensor(ms[m][:, js], pair[m][:, js, 0], pair[m][:, js, 1], ALU.add)
+            for js in parts:
+                nc.vector.tensor_tensor(ratio[m][:, js], ms[m][:, js], inv_ex[m][:, js], ALU.mult)
+
+        def finish(m, js):
+            nc.scalar.activation(res[m][:, js], ratio[m][:, js], ACT.Ln, bias=1.0)
+            nc.sync.dma_start(out[m * P : (m + 1) * P, js], res[m][:, js])
+
+        whole = slice(0, S)
+        halves = [slice(0, HALF), slice(HALF, S)]
+        fifths = [(0, 26), (26, 52), (52, 78), (78, 104), (104, 128)]
+        fetch(0, fifths, True)
+        fetch(1, fifths, False)
+        sums(0, halves)
+        fetch(2, fifths[:2], True)
+        finish(0, whole)
+        sums(1, halves)
+        finish(1, whole)
+        fetch(2, fifths[2:4], True)
+        fetch(2, fifths[4:], False)
+        fetch(3, [(0, 22), (22, 44), (44, 64), (64, 80), (80, 96), (96, 112), (112, 128)], False)
+        sums(2, halves)
+        finish(2, whole)
+        sums(3, [slice(0, 128), slice(128, 256)])
+        finish(3, halves[0])
+        sums(3, [slice(256, 384), slice(384, 512)])
+        finish(3, halves[1])

@@ -1,6 +1,7 @@
 from contextlib import ExitStack
 
 import concourse.mybir as mybir
+from concourse.masks import make_identity
 
 K, T, S, N, H, W, G = 512, 2048, 512, 512, 512, 256, 2048
 P = 128
@@ -78,13 +79,19 @@ def tile_picked_hmixliftglse_none_p_kernel(
         nc.sync.dma_start(w2_raw[:], w2.rearrange("(p j) c -> p j c", j=PACK))
         xq_words = pick_words(l_offs, "xq_words")
 
+        ident = sb.tile([P, P], F32, name="ident")
+        make_identity(nc, ident[:])
         w1_bf = sb.tile([P, PACK, P, PACK], BF16, name="w1_bf", align_bytes=64)
-        for u, copy in enumerate((nc.scalar.copy, nc.vector.tensor_copy)):
+        for copy, u, a, b in (
+            (nc.scalar.copy, 0, 0, 64),
+            (nc.vector.tensor_copy, 1, 0, 44),
+            (nc.scalar.copy, 1, 44, 64),
+        ):
             copy(
-                w1_bf[:, :, u * 64 : (u + 1) * 64, :].rearrange("p t m j -> p m t j"),
-                w1_raw[u][:].rearrange("p j (m t) -> p m t j", t=PACK),
+                w1_bf[:, :, u * 64 + a : u * 64 + b, :].rearrange("p t m j -> p m t j"),
+                w1_raw[u][:].rearrange("p j (m t) -> p m t j", t=PACK)[:, a:b],
             )
-        gain = sb.tile([P, PACK], F32, name="gain", tag="w1_raw0")
+        gain = sb.tile([P, PACK], F32, name="gain", tag="w1_raw1")
         nc.sync.dma_start(gain[:], gn.rearrange("(p t) o -> p (t o)", t=PACK))
         w1_codes = sb.tile([P, H], U32, name="w1_codes", align_bytes=64)
         w1_scales = sb.tile([P, H], U8, name="w1_scales", align_bytes=64)
@@ -99,24 +106,32 @@ def tile_picked_hmixliftglse_none_p_kernel(
 
         neg_pa, pb = [], []
         for t in range(PACK):
-            acc = psum.tile([P, S], F32, name="y_acc%d" % t)
-            nc.tensor.matmul_mx(
-                out=acc[:],
-                lhsT=w1_codes[:, t * P : (t + 1) * P].bitcast(FP8X4),
-                lhsT_scale=w1_scales[:, t * P : (t + 1) * P],
-                rhs=xq_words[:].bitcast(FP8X4),
-                rhs_scale=xq_scales[:],
-                start=True,
-                stop=True,
-            )
             y = sb.tile([P, S], F32, name="y%d" % t)
-            nc.scalar.copy(y[:], acc[:])
+            if t == 0:
+                parts = ((0, HALF, "bank0", nc.scalar.copy), (HALF, S, "bank7", nc.vector.tensor_copy))
+            else:
+                parts = ((0, S, "bank%d" % t, nc.scalar.copy),)
+            for lo, hi, bank, copy in parts:
+                acc = psum.tile([P, hi - lo], F32, name="y_acc%d_%d" % (t, lo), tag=bank)
+                nc.tensor.matmul_mx(
+                    out=acc[:],
+                    lhsT=w1_codes[:, t * P : (t + 1) * P].bitcast(FP8X4),
+                    lhsT_scale=w1_scales[:, t * P : (t + 1) * P],
+                    rhs=xq_words[:, lo:hi].bitcast(FP8X4),
+                    rhs_scale=xq_scales[:, lo:hi],
+                    start=True,
+                    stop=True,
+                )
+                copy(y[:, lo:hi], acc[:])
             a = sb.tile([P, W], F32, name="neg_pa%d" % t)
             b = sb.tile([P, W], F32, name="pb%d" % t)
-            nc.scalar.activation(a[:], y[:].indirect(l_n1[:]), ACT.Copy, scale=-1.0)
             if t == 0:
-                nc.vector.tensor_copy(b[:], y[:].indirect(l_n2[:]))
+                nc.vector.tensor_copy(b[:, 0:128], y[:].indirect(l_n2[:, 0:8]))
+                nc.scalar.activation(a[:, 0:128], y[:].indirect(l_n1[:, 0:8]), ACT.Copy, scale=-1.0)
+                nc.scalar.activation(a[:, 128:256], y[:].indirect(l_n1[:, 8:16]), ACT.Copy, scale=-1.0)
+                nc.scalar.activation(b[:, 128:256], y[:].indirect(l_n2[:, 8:16]), ACT.Copy)
             else:
+                nc.scalar.activation(a[:], y[:].indirect(l_n1[:]), ACT.Copy, scale=-1.0)
                 nc.scalar.activation(b[:], y[:].indirect(l_n2[:]), ACT.Copy)
             neg_pa.append(a)
             pb.append(b)
@@ -129,14 +144,6 @@ def tile_picked_hmixliftglse_none_p_kernel(
             )
             return bf
 
-        def quantize_weight(bf, name):
-            codes = sb.tile([P, N], U32, name=name + "_codes", align_bytes=64)
-            scales = sb.tile([P, N], U8, name=name + "_scales", align_bytes=64)
-            nc.vector.quantize_mx(
-                out=codes[:].bitcast(FP8X4), scales=scales[:], in_=bf[:].rearrange("p c j -> p (c j)")
-            )
-            return codes, scales
-
         w3_bf = round_weight(w3_raw, "w3")
         w2_bf = round_weight(w2_raw, "w2")
 
@@ -145,8 +152,11 @@ def tile_picked_hmixliftglse_none_p_kernel(
         z_pairs = [sb.tile([P, 2, HALF, 2], BF16, name="z_pairs%d" % u, tag="z_pairs%d" % u, align_bytes=64) for u in range(2)]
 
         def put_ra(t):
+            for lo, hi in ((0, 128), (128, 256)) if t == 0 else ((0, 256),):
+                nc.vector.tensor_tensor(
+                    dt[t][:].indirect(l_n1[:, lo // 16 : hi // 16]), pb[t][:, lo:hi], neg_pa[t][:, lo:hi], ALU.add
+                )
             nc.vector.scalar_tensor_tensor(rb[t][:], neg_pa[t][:], -0.5, pb[t][:], ALU.mult, ALU.max)
-            nc.vector.tensor_tensor(dt[t][:].indirect(l_n1[:]), pb[t][:], neg_pa[t][:], ALU.add)
 
         def put_rb(t):
             nc.vector.tensor_copy(dt[t][:].indirect(l_n2[:]), rb[t][:])
@@ -164,11 +174,18 @@ def tile_picked_hmixliftglse_none_p_kernel(
             put_rb(t - 1)
         put_rb(PACK - 1)
 
-        w3_codes, w3_scales = quantize_weight(w3_bf, "w3")
-        w2_flat = w2_bf[:].rearrange("p c j -> p (c j)")
-        w2_first = sb.tile([P, P], U32, name="w2_first", align_bytes=64)
-        w2_scales = sb.tile([P, N], U8, name="w2_scales", align_bytes=64)
-        nc.vector.quantize_mx(out=w2_first[:].bitcast(FP8X4), scales=w2_scales[:, 0:P], in_=w2_flat[:, 0 : PACK * P])
+        def quantize_columns(bf, name, lo, hi, tag):
+            codes = sb.tile([P, hi - lo], U32, name=name + "_codes", tag=tag, align_bytes=64)
+            scales = sb.tile([P, hi - lo], U8, name=name + "_scales", align_bytes=64)
+            nc.vector.quantize_mx(
+                out=codes[:].bitcast(FP8X4),
+                scales=scales[:],
+                in_=bf[:].rearrange("p c j -> p (c j)")[:, PACK * lo : PACK * hi],
+            )
+            return [(codes[:, i : i + P].bitcast(FP8X4), scales[:, i : i + P]) for i in range(0, hi - lo, P)]
+
+        w3_q = quantize_columns(w3_bf, "w3_first", 0, P, "w3_first")
+        w2_q = quantize_columns(w2_bf, "w2_first", 0, P, "w2_first")
 
         z_bf = [sb.tile([P, HALF, PACK], BF16, name="z_bf%d" % u, align_bytes=64) for u in range(2)]
         z_codes = [sb.tile([P, HALF], U32, name="z_codes%d" % u, align_bytes=64) for u in range(2)]
@@ -185,44 +202,57 @@ def tile_picked_hmixliftglse_none_p_kernel(
                 in_=z_bf[u][:].rearrange("p j t -> p (j t)"),
             )
 
-        w2_rest = sb.tile([P, N - P], U32, name="w2_rest", tag="z_pairs1", align_bytes=64)
-        nc.vector.quantize_mx(out=w2_rest[:].bitcast(FP8X4), scales=w2_scales[:, P:N], in_=w2_flat[:, PACK * P :])
-        w2_codes = [w2_first[:]] + [w2_rest[:, i * P : (i + 1) * P] for i in range(3)]
+        w3_q = w3_q + quantize_columns(w3_bf, "w3_rest", P, N, "z_pairs1")
+        w2_q = w2_q + quantize_columns(w2_bf, "w2_rest", P, N, "z_pairs0")
 
-        h_acc = [psum.tile([P, S], F32, name="h_acc%d" % m) for m in range(4)]
+        h_parts = []
         for m in range(4):
-            nc.tensor.matmul_mx(
-                out=h_acc[m][:],
-                lhsT=w3_codes[:, m * P : (m + 1) * P].bitcast(FP8X4),
-                lhsT_scale=w3_scales[:, m * P : (m + 1) * P],
-                rhs=x2_words[:].bitcast(FP8X4),
-                rhs_scale=x2_scales[:],
-                start=True,
-                stop=False,
-            )
-            for u in range(2):
+            if m == 0:
+                spans = ((0, HALF, "bank4"), (HALF, S, "bank3"))
+            else:
+                spans = ((0, S, "bank%d" % (4 + m)),)
+            parts = []
+            for lo, hi, bank in spans:
+                acc = psum.tile([P, hi - lo], F32, name="h_acc%d_%d" % (m, lo), tag=bank)
                 nc.tensor.matmul_mx(
-                    out=h_acc[m][:, u * HALF : (u + 1) * HALF],
-                    lhsT=w2_codes[m].bitcast(FP8X4),
-                    lhsT_scale=w2_scales[:, m * P : (m + 1) * P],
-                    rhs=z_codes[u][:].bitcast(FP8X4),
-                    rhs_scale=z_scales[u][:],
-                    start=False,
-                    stop=(u == 1),
+                    out=acc[:],
+                    lhsT=w3_q[m][0],
+                    lhsT_scale=w3_q[m][1],
+                    rhs=x2_words[:, lo:hi].bitcast(FP8X4),
+                    rhs_scale=x2_scales[:, lo:hi],
+                    start=True,
+                    stop=False,
                 )
+                for c in range(lo, hi, HALF):
+                    nc.tensor.matmul_mx(
+                        out=acc[:, c - lo : c - lo + HALF],
+                        lhsT=w2_q[m][0],
+                        lhsT_scale=w2_q[m][1],
+                        rhs=z_codes[c // HALF][:].bitcast(FP8X4),
+                        rhs_scale=z_scales[c // HALF][:],
+                        start=False,
+                        stop=(c + HALF == hi),
+                    )
+                parts.append((slice(lo, hi), acc))
+            h_parts.append(parts)
 
         ex = [sb.tile([P, S], F32, name="ex%d" % m) for m in range(4)]
-        inv_ex = [sb.tile([P, S], F32, name="inv_ex%d" % m) for m in range(4)]
+        side = [sb.tile([P, S], F32, name="side%d" % m) for m in range(4)]
         mb = [sb.tile([P, G], F32, name="mb%d" % m) for m in range(4)]
-        pair = [sb.tile([P, S, 2], F32, name="pair%d" % m) for m in range(4)]
-        ms = [sb.tile([P, S], F32, name="ms%d" % m) for m in range(4)]
-        ratio = [sb.tile([P, S], F32, name="ratio%d" % m) for m in range(4)]
         res = [sb.tile([P, S], F32, name="res%d" % m) for m in range(4)]
+        pair = {m: sb.tile([P, S, 2], F32, name="pair%d" % m) for m in (2, 3)}
+        ms = {m: sb.tile([P, S], F32, name="ms%d" % m) for m in (2, 3)}
+        ratio = {m: sb.tile([P, S], F32, name="ratio%d" % m) for m in (2, 3)}
+        total = {m: psum.tile([P, S], F32, name="total%d" % m, tag="bank%d" % m) for m in (0, 1)}
 
         for m in range(4):
-            nc.scalar.activation(ex[m][:], h_acc[m][:], ACT.Exp)
-        for m in range(4):
-            nc.scalar.activation(inv_ex[m][:], h_acc[m][:], ACT.Exp, scale=-1.0)
+            for js, acc in h_parts[m]:
+                nc.scalar.activation(ex[m][:, js], acc[:], ACT.Exp)
+            for js, acc in h_parts[m]:
+                if m < 2:
+                    nc.scalar.copy(side[m][:, js], acc[:])
+                else:
+                    nc.scalar.activation(side[m][:, js], acc[:], ACT.Exp, scale=-1.0)
 
         def fetch(m, cols, on_vector):
             for a, b in cols:
@@ -240,26 +270,52 @@ def tile_picked_hmixliftglse_none_p_kernel(
             for js in parts:
                 nc.vector.tensor_tensor(ms[m][:, js], pair[m][:, js, 0], pair[m][:, js, 1], ALU.add)
             for js in parts:
-                nc.vector.tensor_tensor(ratio[m][:, js], ms[m][:, js], inv_ex[m][:, js], ALU.mult)
+                nc.vector.tensor_tensor(ratio[m][:, js], ms[m][:, js], side[m][:, js], ALU.mult)
 
         def finish(m, js):
             nc.scalar.activation(res[m][:, js], ratio[m][:, js], ACT.Ln, bias=1.0)
             nc.sync.dma_start(out[m * P : (m + 1) * P, js], res[m][:, js])
 
+        def sums_turned(m):
+            members = mb[m][:].rearrange("p (j t) -> p j t", t=MEMBERS)
+            for b in range(4):
+                js = slice(b * P, (b + 1) * P)
+                terms = [ex[m][:, js]] + [members[:, js, t] for t in range(MEMBERS)]
+                for i, term in enumerate(terms):
+                    nc.tensor.matmul(
+                        total[m][:, js], lhsT=term, rhs=ident[:], is_transpose=True,
+                        start=(i == 0), stop=(i == MEMBERS),
+                    )
+
+        def log_turned(m):
+            logs = sb.tile([P, S], F32, name="logs%d" % m)
+            nc.scalar.activation(logs[:], total[m][:], ACT.Ln)
+            back = psum.tile([P, S], F32, name="back%d" % m, tag="bank%d" % (2 + m))
+            for b in range(4):
+                js = slice(b * P, (b + 1) * P)
+                nc.tensor.transpose(back[:, js], logs[:, js], ident[:])
+            return back
+
+        def finish_turned(m, back):
+            nc.vector.tensor_tensor(res[m][:], back[:], side[m][:], ALU.subtract)
+            nc.sync.dma_start(out[m * P : (m + 1) * P, :], res[m][:])
+
         whole = slice(0, S)
         halves = [slice(0, HALF), slice(HALF, S)]
+        eighths = [(16 * i, 16 * i + 16) for i in range(8)]
         fifths = [(0, 26), (26, 52), (52, 78), (78, 104), (104, 128)]
-        fetch(0, fifths, True)
-        fetch(1, fifths, False)
-        sums(0, halves)
-        fetch(2, fifths[:2], True)
-        finish(0, whole)
-        sums(1, halves)
-        finish(1, whole)
-        fetch(2, fifths[2:4], True)
-        fetch(2, fifths[4:], False)
-        fetch(3, [(0, 22), (22, 44), (44, 64), (64, 80), (80, 96), (96, 112), (112, 128)], False)
+        fetch(0, eighths, True)
+        sums_turned(0)
+        fetch(1, eighths, False)
+        sums_turned(1)
+        fetch(2, fifths, True)
+        back0 = log_turned(0)
+        back1 = log_turned(1)
         sums(2, halves)
+        fetch(3, fifths[:1], True)
+        fetch(3, [(26, 46), (46, 64), (64, 80), (80, 96), (96, 112), (112, 128)], False)
+        finish_turned(0, back0)
+        finish_turned(1, back1)
         finish(2, whole)
         sums(3, [slice(0, 128), slice(128, 256)])
         finish(3, halves[0])

@@ -20,6 +20,8 @@ ALU = mybir.AluOpType
 
 HALF = S // 2
 MEMBERS = G // S
+TURN2 = HALF
+SPARE = 32
 
 
 def tile_picked_hmixliftglse_none_p_kernel(
@@ -50,7 +52,7 @@ def tile_picked_hmixliftglse_none_p_kernel(
         w1_rows = w1.rearrange("(p j) c -> p j c", j=PACK)
         w1_raw = []
         for u in range(2):
-            t = sb.tile([P, PACK, H // 2], F32, name="w1_raw%d" % u, tag="w1_raw%d" % u)
+            t = sb.tile([P, PACK, H // 2], F32, name="w1_raw%d" % u, tag="w1_raw%d" % u, align_bytes=64)
             nc.sync.dma_start(t[:], w1_rows[:, :, u * (H // 2) : (u + 1) * (H // 2)])
             w1_raw.append(t)
         l_n3 = load_list(n3, "l_n3")
@@ -66,9 +68,9 @@ def tile_picked_hmixliftglse_none_p_kernel(
                 )
             return placed
 
-        def pick_words(lst, name):
-            picked = sb.tile([P, S], U32, name=name, align_bytes=64)
-            nc.vector.tensor_copy(picked[:], xw[:].bitcast(U32).indirect(lst[:]))
+        def pick_words(offsets, name, tag):
+            picked = sb.tile([P, 16 * offsets.shape[1]], U32, name=name, tag=tag, align_bytes=64)
+            nc.vector.tensor_copy(picked[:], xw[:].bitcast(U32).indirect(offsets))
             return picked
 
         xq_scales = pick_scales(l_offs, "xq_s", nc.scalar)
@@ -77,7 +79,8 @@ def tile_picked_hmixliftglse_none_p_kernel(
         nc.sync.dma_start(w3_raw[:], w3.rearrange("(p j) c -> p j c", j=PACK))
         w2_raw = sb.tile([P, PACK, N], F32, name="w2_raw", tag="x2_s_late", align_bytes=64)
         nc.sync.dma_start(w2_raw[:], w2.rearrange("(p j) c -> p j c", j=PACK))
-        xq_words = pick_words(l_offs, "xq_words")
+        xq_words = pick_words(l_offs[:], "xq_words", "xq_words")
+        x2_words = [pick_words(l_two[:, 0:16], "x2_words0", "x2_words0")]
 
         ident = sb.tile([P, P], F32, name="ident")
         make_identity(nc, ident[:])
@@ -91,7 +94,7 @@ def tile_picked_hmixliftglse_none_p_kernel(
                 w1_bf[:, :, u * 64 + a : u * 64 + b, :].rearrange("p t m j -> p m t j"),
                 w1_raw[u][:].rearrange("p j (m t) -> p m t j", t=PACK)[:, a:b],
             )
-        gain = sb.tile([P, PACK], F32, name="gain", tag="w1_raw1")
+        gain = sb.tile([P, PACK], F32, name="gain", tag="w1_raw0", align_bytes=64)
         nc.sync.dma_start(gain[:], gn.rearrange("(p t) o -> p (t o)", t=PACK))
         w1_codes = sb.tile([P, H], U32, name="w1_codes", align_bytes=64)
         w1_scales = sb.tile([P, H], U8, name="w1_scales", align_bytes=64)
@@ -102,7 +105,7 @@ def tile_picked_hmixliftglse_none_p_kernel(
                 scales=w1_scales[:, a:b],
                 in_=w1_flat[:, PACK * a : PACK * b],
             )
-        x2_words = pick_words(l_two, "x2_words")
+        x2_words.append(pick_words(l_two[:, 16:32], "x2_words1", "w1_raw1"))
 
         neg_pa, pb = [], []
         for t in range(PACK):
@@ -136,16 +139,12 @@ def tile_picked_hmixliftglse_none_p_kernel(
             neg_pa.append(a)
             pb.append(b)
 
-        def round_weight(raw, name):
-            bf = sb.tile([P, N, PACK], BF16, name=name + "_bf", align_bytes=64)
+        w_bf = sb.tile([P, 4, 2, P, PACK], BF16, name="w_bf", align_bytes=64)
+        for which, raw in enumerate((w3_raw, w2_raw)):
             nc.scalar.copy(
-                bf[:].rearrange("p (c i) j -> p c j i", i=4),
-                raw[:].rearrange("p j (c i) -> p c j i", i=4),
+                w_bf[:, :, which].rearrange("p m (c i) j -> p m c j i", i=4),
+                raw[:].rearrange("p j (m c i) -> p m c j i", m=4, i=4),
             )
-            return bf
-
-        w3_bf = round_weight(w3_raw, "w3")
-        w2_bf = round_weight(w2_raw, "w2")
 
         dt = [sb.tile([P, S], F32, name="dt%d" % t) for t in range(PACK)]
         rb = [sb.tile([P, W], F32, name="rb%d" % t) for t in range(PACK)]
@@ -174,18 +173,18 @@ def tile_picked_hmixliftglse_none_p_kernel(
             put_rb(t - 1)
         put_rb(PACK - 1)
 
-        def quantize_columns(bf, name, lo, hi, tag):
-            codes = sb.tile([P, hi - lo], U32, name=name + "_codes", tag=tag, align_bytes=64)
-            scales = sb.tile([P, hi - lo], U8, name=name + "_scales", align_bytes=64)
+        def quantize_weights(name, lo, hi, tag):
+            width = 2 * P * (hi - lo)
+            codes = sb.tile([P, width], U32, name=name + "_codes", tag=tag, align_bytes=64)
+            scales = sb.tile([P, width], U8, name=name + "_scales", align_bytes=64)
             nc.vector.quantize_mx(
                 out=codes[:].bitcast(FP8X4),
                 scales=scales[:],
-                in_=bf[:].rearrange("p c j -> p (c j)")[:, PACK * lo : PACK * hi],
+                in_=w_bf[:, lo:hi].rearrange("p m w c j -> p (m w c j)"),
             )
-            return [(codes[:, i : i + P].bitcast(FP8X4), scales[:, i : i + P]) for i in range(0, hi - lo, P)]
+            return [(codes[:, i : i + P].bitcast(FP8X4), scales[:, i : i + P]) for i in range(0, width, P)]
 
-        w3_q = quantize_columns(w3_bf, "w3_first", 0, P, "w3_first")
-        w2_q = quantize_columns(w2_bf, "w2_first", 0, P, "w2_first")
+        w_q = quantize_weights("w_first", 0, 2, "w_first")
 
         z_bf = [sb.tile([P, HALF, PACK], BF16, name="z_bf%d" % u, align_bytes=64) for u in range(2)]
         z_codes = [sb.tile([P, HALF], U32, name="z_codes%d" % u, align_bytes=64) for u in range(2)]
@@ -202,8 +201,7 @@ def tile_picked_hmixliftglse_none_p_kernel(
                 in_=z_bf[u][:].rearrange("p j t -> p (j t)"),
             )
 
-        w3_q = w3_q + quantize_columns(w3_bf, "w3_rest", P, N, "z_pairs1")
-        w2_q = w2_q + quantize_columns(w2_bf, "w2_rest", P, N, "z_pairs0")
+        w_q = w_q + quantize_weights("w_rest", 2, 4, "z_pairs1")
 
         h_parts = []
         for m in range(4):
@@ -214,20 +212,21 @@ def tile_picked_hmixliftglse_none_p_kernel(
             parts = []
             for lo, hi, bank in spans:
                 acc = psum.tile([P, hi - lo], F32, name="h_acc%d_%d" % (m, lo), tag=bank)
-                nc.tensor.matmul_mx(
-                    out=acc[:],
-                    lhsT=w3_q[m][0],
-                    lhsT_scale=w3_q[m][1],
-                    rhs=x2_words[:, lo:hi].bitcast(FP8X4),
-                    rhs_scale=x2_scales[:, lo:hi],
-                    start=True,
-                    stop=False,
-                )
                 for c in range(lo, hi, HALF):
                     nc.tensor.matmul_mx(
                         out=acc[:, c - lo : c - lo + HALF],
-                        lhsT=w2_q[m][0],
-                        lhsT_scale=w2_q[m][1],
+                        lhsT=w_q[2 * m][0],
+                        lhsT_scale=w_q[2 * m][1],
+                        rhs=x2_words[c // HALF][:].bitcast(FP8X4),
+                        rhs_scale=x2_scales[:, c : c + HALF],
+                        start=(c == lo),
+                        stop=False,
+                    )
+                for c in range(lo, hi, HALF):
+                    nc.tensor.matmul_mx(
+                        out=acc[:, c - lo : c - lo + HALF],
+                        lhsT=w_q[2 * m + 1][0],
+                        lhsT_scale=w_q[2 * m + 1][1],
                         rhs=z_codes[c // HALF][:].bitcast(FP8X4),
                         rhs_scale=z_scales[c // HALF][:],
                         start=False,
@@ -236,25 +235,28 @@ def tile_picked_hmixliftglse_none_p_kernel(
                 parts.append((slice(lo, hi), acc))
             h_parts.append(parts)
 
-        ex = [sb.tile([P, S], F32, name="ex%d" % m) for m in range(4)]
+        ex = [sb.tile([P, S + SPARE], F32, name="ex%d" % m) for m in range(4)]
+        for m in range(4):
+            nc.gpsimd.memset(ex[m][:, S:], 0.0)
         side = [sb.tile([P, S], F32, name="side%d" % m) for m in range(4)]
-        mb = [sb.tile([P, G], F32, name="mb%d" % m) for m in range(4)]
         res = [sb.tile([P, S], F32, name="res%d" % m) for m in range(4)]
-        pair = {m: sb.tile([P, S, 2], F32, name="pair%d" % m) for m in (2, 3)}
-        ms = {m: sb.tile([P, S], F32, name="ms%d" % m) for m in (2, 3)}
-        ratio = {m: sb.tile([P, S], F32, name="ratio%d" % m) for m in (2, 3)}
-        total = {m: psum.tile([P, S], F32, name="total%d" % m, tag="bank%d" % m) for m in (0, 1)}
+        turned = (S, S, TURN2, 0)
 
         for m in range(4):
             for js, acc in h_parts[m]:
                 nc.scalar.activation(ex[m][:, js], acc[:], ACT.Exp)
             for js, acc in h_parts[m]:
-                if m < 2:
-                    nc.scalar.copy(side[m][:, js], acc[:])
-                else:
-                    nc.scalar.activation(side[m][:, js], acc[:], ACT.Exp, scale=-1.0)
+                cut = min(max(turned[m], js.start), js.stop)
+                if cut > js.start:
+                    nc.scalar.copy(side[m][:, js.start : cut], acc[:, 0 : cut - js.start])
+                if cut < js.stop:
+                    nc.scalar.activation(side[m][:, cut : js.stop], acc[:, cut - js.start :], ACT.Exp, scale=-1.0)
+
+        mb = {}
 
         def fetch(m, cols, on_vector):
+            if m not in mb:
+                mb[m] = sb.tile([P, G], F32, name="mb%d" % m, tag="mb%d" % (m % 3))
             for a, b in cols:
                 dst = mb[m][:, 16 * a : 16 * b]
                 src = ex[m][:].indirect(l_n3[:, a:b])
@@ -262,6 +264,10 @@ def tile_picked_hmixliftglse_none_p_kernel(
                     nc.vector.tensor_copy(dst, src)
                 else:
                     nc.scalar.activation(dst, src, ACT.Copy)
+
+        pair = {m: sb.tile([P, S, 2], F32, name="pair%d" % m) for m in (2, 3)}
+        ms = {m: sb.tile([P, S], F32, name="ms%d" % m) for m in (2, 3)}
+        ratio = {m: sb.tile([P, S], F32, name="ratio%d" % m) for m in (2, 3)}
 
         def sums(m, parts):
             members = mb[m][:].rearrange("p (j t) -> p j t", t=MEMBERS)
@@ -276,48 +282,53 @@ def tile_picked_hmixliftglse_none_p_kernel(
             nc.scalar.activation(res[m][:, js], ratio[m][:, js], ACT.Ln, bias=1.0)
             nc.sync.dma_start(out[m * P : (m + 1) * P, js], res[m][:, js])
 
-        def sums_turned(m):
+        def sums_turned(m, bank):
+            total = psum.tile([P, turned[m]], F32, name="total%d" % m, tag=bank)
             members = mb[m][:].rearrange("p (j t) -> p j t", t=MEMBERS)
-            for b in range(4):
-                js = slice(b * P, (b + 1) * P)
+            for lo in range(0, turned[m], P):
+                js = slice(lo, lo + P)
                 terms = [ex[m][:, js]] + [members[:, js, t] for t in range(MEMBERS)]
                 for i, term in enumerate(terms):
                     nc.tensor.matmul(
-                        total[m][:, js], lhsT=term, rhs=ident[:], is_transpose=True,
+                        total[:, js], lhsT=term, rhs=ident[:], is_transpose=True,
                         start=(i == 0), stop=(i == MEMBERS),
                     )
+            return total
 
-        def log_turned(m):
-            logs = sb.tile([P, S], F32, name="logs%d" % m)
-            nc.scalar.activation(logs[:], total[m][:], ACT.Ln)
-            back = psum.tile([P, S], F32, name="back%d" % m, tag="bank%d" % (2 + m))
-            for b in range(4):
-                js = slice(b * P, (b + 1) * P)
-                nc.tensor.transpose(back[:, js], logs[:, js], ident[:])
+        def log_turned(m, total, bank):
+            logs = sb.tile([P, turned[m]], F32, name="logs%d" % m)
+            nc.scalar.activation(logs[:], total[:], ACT.Ln)
+            back = psum.tile([P, turned[m]], F32, name="back%d" % m, tag=bank)
+            for lo in range(0, turned[m], P):
+                nc.tensor.transpose(back[:, lo : lo + P], logs[:, lo : lo + P], ident[:])
             return back
 
         def finish_turned(m, back):
-            nc.vector.tensor_tensor(res[m][:], back[:], side[m][:], ALU.subtract)
-            nc.sync.dma_start(out[m * P : (m + 1) * P, :], res[m][:])
+            js = slice(0, turned[m])
+            nc.vector.tensor_tensor(res[m][:, js], back[:], side[m][:, js], ALU.subtract)
+            nc.sync.dma_start(out[m * P : (m + 1) * P, js], res[m][:, js])
 
-        whole = slice(0, S)
         halves = [slice(0, HALF), slice(HALF, S)]
-        eighths = [(16 * i, 16 * i + 16) for i in range(8)]
-        fifths = [(0, 26), (26, 52), (52, 78), (78, 104), (104, 128)]
-        fetch(0, eighths, True)
-        sums_turned(0)
-        fetch(1, eighths, False)
-        sums_turned(1)
-        fetch(2, fifths, True)
-        back0 = log_turned(0)
-        back1 = log_turned(1)
-        sums(2, halves)
-        fetch(3, fifths[:1], True)
-        fetch(3, [(26, 46), (46, 64), (64, 80), (80, 96), (96, 112), (112, 128)], False)
+        quarters = [slice(i * P, (i + 1) * P) for i in range(4)]
+        blocks = [(32 * i, 32 * i + 32) for i in range(4)]
+        fetch(0, blocks, True)
+        total0 = sums_turned(0, "bank0")
+        fetch(1, blocks, False)
+        total1 = sums_turned(1, "bank1")
+        fetch(2, blocks, True)
+        total2 = sums_turned(2, "bank4")
+        back0 = log_turned(0, total0, "bank2")
+        back1 = log_turned(1, total1, "bank3")
+        back2 = log_turned(2, total2, "bank5")
+        fetch(3, [(0, 24)], True)
+        fetch(3, [(24, 44), (44, 64), (64, 96), (96, 128)], False)
         finish_turned(0, back0)
+        sums(2, halves[1:])
+        finish(2, halves[1])
         finish_turned(1, back1)
-        finish(2, whole)
-        sums(3, [slice(0, 128), slice(128, 256)])
+        finish_turned(2, back2)
+        sums(3, halves[:1])
         finish(3, halves[0])
-        sums(3, [slice(256, 384), slice(384, 512)])
-        finish(3, halves[1])
+        sums(3, quarters[2:])
+        finish(3, quarters[2])
+        finish(3, quarters[3])

from contextlib import ExitStack

import concourse.mybir as mybir
from concourse.masks import make_identity

K, T, S, N, H, W, G = 512, 2048, 512, 512, 512, 256, 2048
P = 128
PACK = 4
FLOPS = 2 * (K * H * S + H * N * S + K * N * S)

F32 = mybir.dt.float32
BF16 = mybir.dt.bfloat16
I32 = mybir.dt.int32
U32 = mybir.dt.uint32
U16 = mybir.dt.uint16
U8 = mybir.dt.uint8
FP8X4 = mybir.dt.float8_e4m3fn_x4
ACT = mybir.ActivationFunctionType
ALU = mybir.AluOpType

HALF = S // 2
MEMBERS = G // S
TURN2 = HALF
SPARE = 32


def tile_picked_hmixliftglse_none_p_kernel(
    tc, x_words, x_scales, w1, gn, w2, w3, offs, n1, n2, two, n3, out
):
    nc = tc.nc
    with ExitStack() as ctx:
        lists = ctx.enter_context(tc.tile_pool(name="lists", bufs=1))
        sb = ctx.enter_context(tc.tile_pool(name="sb", bufs=1))
        psum = ctx.enter_context(tc.psum_pool(name="psum", bufs=1))

        def load_list(src, name):
            t = lists.tile(list(src.shape), U16, name=name)
            nc.sync.dma_start(t[:], src)
            return t

        l_offs = load_list(offs, "l_offs")
        xs = sb.tile([P, T], U8, name="xs", align_bytes=64)
        nc.sync.dma_start(
            xs[:].bitcast(I32),
            x_scales[0].bitcast(I32).unsqueeze(1).to_broadcast([16, 8, T // 4]),
        )
        l_two = load_list(two, "l_two")
        l_n1 = load_list(n1, "l_n1")
        l_n2 = load_list(n2, "l_n2")
        xw = sb.tile([P, T], I32, name="xw", align_bytes=64)
        nc.sync.dma_start(xw[:], x_words[0].rearrange("p n t -> p (n t)").bitcast(I32))
        w1_rows = w1.rearrange("(p j) c -> p j c", j=PACK)
        w1_raw = []
        for u in range(2):
            t = sb.tile([P, PACK, H // 2], F32, name="w1_raw%d" % u, tag="w1_raw%d" % u, align_bytes=64)
            nc.sync.dma_start(t[:], w1_rows[:, :, u * (H // 2) : (u + 1) * (H // 2)])
            w1_raw.append(t)
        l_n3 = load_list(n3, "l_n3")

        def pick_scales(lst, name, queue):
            placed = sb.tile([P, S], U8, name=name + "_placed", align_bytes=64)
            nc.gpsimd.memset(placed[:], 0)
            picked = sb.tile([P, S], U8, name=name + "_picked", tag=name + "_late", align_bytes=64)
            nc.vector.tensor_copy(picked[:], xs[:].indirect(lst[:]))
            for r in range(4):
                queue.dma_start(
                    placed[r:P:32, :].bitcast(I32), picked[8 * r : P : 32, :].bitcast(I32)
                )
            return placed

        def pick_words(offsets, name, tag):
            picked = sb.tile([P, 16 * offsets.shape[1]], U32, name=name, tag=tag, align_bytes=64)
            nc.vector.tensor_copy(picked[:], xw[:].bitcast(U32).indirect(offsets))
            return picked

        xq_scales = pick_scales(l_offs, "xq_s", nc.scalar)
        x2_scales = pick_scales(l_two, "x2_s", nc.sync)
        w3_raw = sb.tile([P, PACK, N], F32, name="w3_raw", tag="xq_s_late", align_bytes=64)
        nc.sync.dma_start(w3_raw[:], w3.rearrange("(p j) c -> p j c", j=PACK))
        w2_raw = sb.tile([P, PACK, N], F32, name="w2_raw", tag="x2_s_late", align_bytes=64)
        nc.sync.dma_start(w2_raw[:], w2.rearrange("(p j) c -> p j c", j=PACK))
        xq_words = pick_words(l_offs[:], "xq_words", "xq_words")
        x2_words = [pick_words(l_two[:, 0:16], "x2_words0", "x2_words0")]

        ident = sb.tile([P, P], F32, name="ident")
        make_identity(nc, ident[:])
        w1_bf = sb.tile([P, PACK, P, PACK], BF16, name="w1_bf", align_bytes=64)
        for copy, u, a, b in (
            (nc.scalar.copy, 0, 0, 64),
            (nc.vector.tensor_copy, 1, 0, 44),
            (nc.scalar.copy, 1, 44, 64),
        ):
            copy(
                w1_bf[:, :, u * 64 + a : u * 64 + b, :].rearrange("p t m j -> p m t j"),
                w1_raw[u][:].rearrange("p j (m t) -> p m t j", t=PACK)[:, a:b],
            )
        gain = sb.tile([P, PACK], F32, name="gain", tag="w1_raw0", align_bytes=64)
        nc.sync.dma_start(gain[:], gn.rearrange("(p t) o -> p (t o)", t=PACK))
        w1_codes = sb.tile([P, H], U32, name="w1_codes", align_bytes=64)
        w1_scales = sb.tile([P, H], U8, name="w1_scales", align_bytes=64)
        w1_flat = w1_bf[:].rearrange("p t m j -> p (t m j)")
        for a, b in ((0, P), (P, H)):
            nc.vector.quantize_mx(
                out=w1_codes[:, a:b].bitcast(FP8X4),
                scales=w1_scales[:, a:b],
                in_=w1_flat[:, PACK * a : PACK * b],
            )
        x2_words.append(pick_words(l_two[:, 16:32], "x2_words1", "w1_raw1"))

        neg_pa, pb = [], []
        for t in range(PACK):
            y = sb.tile([P, S], F32, name="y%d" % t)
            if t == 0:
                parts = ((0, HALF, "bank0", nc.scalar.copy), (HALF, S, "bank7", nc.vector.tensor_copy))
            else:
                parts = ((0, S, "bank%d" % t, nc.scalar.copy),)
            for lo, hi, bank, copy in parts:
                acc = psum.tile([P, hi - lo], F32, name="y_acc%d_%d" % (t, lo), tag=bank)
                nc.tensor.matmul_mx(
                    out=acc[:],
                    lhsT=w1_codes[:, t * P : (t + 1) * P].bitcast(FP8X4),
                    lhsT_scale=w1_scales[:, t * P : (t + 1) * P],
                    rhs=xq_words[:, lo:hi].bitcast(FP8X4),
                    rhs_scale=xq_scales[:, lo:hi],
                    start=True,
                    stop=True,
                )
                copy(y[:, lo:hi], acc[:])
            a = sb.tile([P, W], F32, name="neg_pa%d" % t)
            b = sb.tile([P, W], F32, name="pb%d" % t)
            if t == 0:
                nc.vector.tensor_copy(b[:, 0:128], y[:].indirect(l_n2[:, 0:8]))
                nc.scalar.activation(a[:, 0:128], y[:].indirect(l_n1[:, 0:8]), ACT.Copy, scale=-1.0)
                nc.scalar.activation(a[:, 128:256], y[:].indirect(l_n1[:, 8:16]), ACT.Copy, scale=-1.0)
                nc.scalar.activation(b[:, 128:256], y[:].indirect(l_n2[:, 8:16]), ACT.Copy)
            else:
                nc.scalar.activation(a[:], y[:].indirect(l_n1[:]), ACT.Copy, scale=-1.0)
                nc.scalar.activation(b[:], y[:].indirect(l_n2[:]), ACT.Copy)
            neg_pa.append(a)
            pb.append(b)

        w_bf = sb.tile([P, 4, 2, P, PACK], BF16, name="w_bf", align_bytes=64)
        for which, raw in enumerate((w3_raw, w2_raw)):
            nc.scalar.copy(
                w_bf[:, :, which].rearrange("p m (c i) j -> p m c j i", i=4),
                raw[:].rearrange("p j (m c i) -> p m c j i", m=4, i=4),
            )

        dt = [sb.tile([P, S], F32, name="dt%d" % t) for t in range(PACK)]
        rb = [sb.tile([P, W], F32, name="rb%d" % t) for t in range(PACK)]
        z_pairs = [sb.tile([P, 2, HALF, 2], BF16, name="z_pairs%d" % u, tag="z_pairs%d" % u, align_bytes=64) for u in range(2)]

        def put_ra(t):
            for lo, hi in ((0, 128), (128, 256)) if t == 0 else ((0, 256),):
                nc.vector.tensor_tensor(
                    dt[t][:].indirect(l_n1[:, lo // 16 : hi // 16]), pb[t][:, lo:hi], neg_pa[t][:, lo:hi], ALU.add
                )
            nc.vector.scalar_tensor_tensor(rb[t][:], neg_pa[t][:], -0.5, pb[t][:], ALU.mult, ALU.max)

        def put_rb(t):
            nc.vector.tensor_copy(dt[t][:].indirect(l_n2[:]), rb[t][:])
            for u in range(2):
                nc.scalar.activation(
                    z_pairs[u][:, t // 2, :, t % 2],
                    dt[t][:, u * HALF : (u + 1) * HALF],
                    ACT.Copy,
                    scale=gain[:, t : t + 1],
                )

        put_ra(0)
        for t in range(1, PACK):
            put_ra(t)
            put_rb(t - 1)
        put_rb(PACK - 1)

        def quantize_weights(name, lo, hi, tag):
            width = 2 * P * (hi - lo)
            codes = sb.tile([P, width], U32, name=name + "_codes", tag=tag, align_bytes=64)
            scales = sb.tile([P, width], U8, name=name + "_scales", align_bytes=64)
            nc.vector.quantize_mx(
                out=codes[:].bitcast(FP8X4),
                scales=scales[:],
                in_=w_bf[:, lo:hi].rearrange("p m w c j -> p (m w c j)"),
            )
            return [(codes[:, i : i + P].bitcast(FP8X4), scales[:, i : i + P]) for i in range(0, width, P)]

        w_q = quantize_weights("w_first", 0, 2, "w_first")

        z_bf = [sb.tile([P, HALF, PACK], BF16, name="z_bf%d" % u, align_bytes=64) for u in range(2)]
        z_codes = [sb.tile([P, HALF], U32, name="z_codes%d" % u, align_bytes=64) for u in range(2)]
        z_scales = [sb.tile([P, HALF], U8, name="z_scales%d" % u, align_bytes=64) for u in range(2)]
        for u in range(2):
            nc.vector.tensor_copy(
                z_bf[u][:].rearrange("p j t -> p (j t)").bitcast(F32).rearrange("p (j h) -> p j h", h=2),
                z_pairs[u][:].rearrange("p h j e -> p h (j e)").bitcast(F32).rearrange("p h j -> p j h"),
            )
        for u in range(2):
            nc.vector.quantize_mx(
                out=z_codes[u][:].bitcast(FP8X4),
                scales=z_scales[u][:],
                in_=z_bf[u][:].rearrange("p j t -> p (j t)"),
            )

        w_q = w_q + quantize_weights("w_rest", 2, 4, "z_pairs1")

        h_parts = []
        for m in range(4):
            if m == 0:
                spans = ((0, HALF, "bank4"), (HALF, S, "bank3"))
            else:
                spans = ((0, S, "bank%d" % (4 + m)),)
            parts = []
            for lo, hi, bank in spans:
                acc = psum.tile([P, hi - lo], F32, name="h_acc%d_%d" % (m, lo), tag=bank)
                for c in range(lo, hi, HALF):
                    nc.tensor.matmul_mx(
                        out=acc[:, c - lo : c - lo + HALF],
                        lhsT=w_q[2 * m][0],
                        lhsT_scale=w_q[2 * m][1],
                        rhs=x2_words[c // HALF][:].bitcast(FP8X4),
                        rhs_scale=x2_scales[:, c : c + HALF],
                        start=(c == lo),
                        stop=False,
                    )
                for c in range(lo, hi, HALF):
                    nc.tensor.matmul_mx(
                        out=acc[:, c - lo : c - lo + HALF],
                        lhsT=w_q[2 * m + 1][0],
                        lhsT_scale=w_q[2 * m + 1][1],
                        rhs=z_codes[c // HALF][:].bitcast(FP8X4),
                        rhs_scale=z_scales[c // HALF][:],
                        start=False,
                        stop=(c + HALF == hi),
                    )
                parts.append((slice(lo, hi), acc))
            h_parts.append(parts)

        ex = [sb.tile([P, S + SPARE], F32, name="ex%d" % m) for m in range(4)]
        for m in range(4):
            nc.gpsimd.memset(ex[m][:, S:], 0.0)
        side = [sb.tile([P, S], F32, name="side%d" % m) for m in range(4)]
        res = [sb.tile([P, S], F32, name="res%d" % m) for m in range(4)]
        turned = (S, S, TURN2, 0)

        for m in range(4):
            for js, acc in h_parts[m]:
                nc.scalar.activation(ex[m][:, js], acc[:], ACT.Exp)
            for js, acc in h_parts[m]:
                cut = min(max(turned[m], js.start), js.stop)
                if cut > js.start:
                    nc.scalar.copy(side[m][:, js.start : cut], acc[:, 0 : cut - js.start])
                if cut < js.stop:
                    nc.scalar.activation(side[m][:, cut : js.stop], acc[:, cut - js.start :], ACT.Exp, scale=-1.0)

        mb = {}

        def fetch(m, cols, on_vector):
            if m not in mb:
                mb[m] = sb.tile([P, G], F32, name="mb%d" % m, tag="mb%d" % (m % 3))
            for a, b in cols:
                dst = mb[m][:, 16 * a : 16 * b]
                src = ex[m][:].indirect(l_n3[:, a:b])
                if on_vector:
                    nc.vector.tensor_copy(dst, src)
                else:
                    nc.scalar.activation(dst, src, ACT.Copy)

        pair = {m: sb.tile([P, S, 2], F32, name="pair%d" % m) for m in (2, 3)}
        ms = {m: sb.tile([P, S], F32, name="ms%d" % m) for m in (2, 3)}
        ratio = {m: sb.tile([P, S], F32, name="ratio%d" % m) for m in (2, 3)}

        def sums(m, parts):
            members = mb[m][:].rearrange("p (j t) -> p j t", t=MEMBERS)
            for js in parts:
                nc.vector.tensor_tensor(pair[m][:, js, :], members[:, js, 0:2], members[:, js, 2:4], ALU.add)
            for js in parts:
                nc.vector.tensor_tensor(ms[m][:, js], pair[m][:, js, 0], pair[m][:, js, 1], ALU.add)
            for js in parts:
                nc.vector.tensor_tensor(ratio[m][:, js], ms[m][:, js], side[m][:, js], ALU.mult)

        def finish(m, js):
            nc.scalar.activation(res[m][:, js], ratio[m][:, js], ACT.Ln, bias=1.0)
            nc.sync.dma_start(out[m * P : (m + 1) * P, js], res[m][:, js])

        def sums_turned(m, bank):
            total = psum.tile([P, turned[m]], F32, name="total%d" % m, tag=bank)
            members = mb[m][:].rearrange("p (j t) -> p j t", t=MEMBERS)
            for lo in range(0, turned[m], P):
                js = slice(lo, lo + P)
                terms = [ex[m][:, js]] + [members[:, js, t] for t in range(MEMBERS)]
                for i, term in enumerate(terms):
                    nc.tensor.matmul(
                        total[:, js], lhsT=term, rhs=ident[:], is_transpose=True,
                        start=(i == 0), stop=(i == MEMBERS),
                    )
            return total

        def log_turned(m, total, bank):
            logs = sb.tile([P, turned[m]], F32, name="logs%d" % m)
            nc.scalar.activation(logs[:], total[:], ACT.Ln)
            back = psum.tile([P, turned[m]], F32, name="back%d" % m, tag=bank)
            for lo in range(0, turned[m], P):
                nc.tensor.transpose(back[:, lo : lo + P], logs[:, lo : lo + P], ident[:])
            return back

        def finish_turned(m, back):
            js = slice(0, turned[m])
            nc.vector.tensor_tensor(res[m][:, js], back[:], side[m][:, js], ALU.subtract)
            nc.sync.dma_start(out[m * P : (m + 1) * P, js], res[m][:, js])

        halves = [slice(0, HALF), slice(HALF, S)]
        quarters = [slice(i * P, (i + 1) * P) for i in range(4)]
        blocks = [(32 * i, 32 * i + 32) for i in range(4)]
        fetch(0, blocks, True)
        total0 = sums_turned(0, "bank0")
        fetch(1, blocks, False)
        total1 = sums_turned(1, "bank1")
        fetch(2, blocks, True)
        total2 = sums_turned(2, "bank4")
        back0 = log_turned(0, total0, "bank2")
        back1 = log_turned(1, total1, "bank3")
        back2 = log_turned(2, total2, "bank5")
        fetch(3, [(0, 24)], True)
        fetch(3, [(24, 44), (44, 64), (64, 96), (96, 128)], False)
        finish_turned(0, back0)
        sums(2, halves[1:])
        finish(2, halves[1])
        finish_turned(1, back1)
        finish_turned(2, back2)
        sums(3, halves[:1])
        finish(3, halves[0])
        sums(3, quarters[2:])
        finish(3, quarters[2])
        finish(3, quarters[3])
